import numpy as np
import ml_dtypes


def mxq(x, axis, fmt="e4m3"):
    dtype, down = {"e4m3": (ml_dtypes.float8_e4m3fn, 7), "e5m2": (ml_dtypes.float8_e5m2, 14)}[fmt]
    v = np.moveaxis(np.asarray(x, np.float32).astype(ml_dtypes.bfloat16).astype(np.float64), axis, -1)
    blocks = v.reshape(v.shape[:-1] + (-1, 32))
    amax = np.abs(blocks).max(-1, keepdims=True)
    byte = np.maximum(np.where(amax > 0, np.frexp(amax)[1] - 1 + 127, 0) - down, 1)
    scale = np.exp2(byte - 127.0)
    codes = (blocks / scale).astype(np.float32).astype(dtype).astype(np.float64)
    return np.moveaxis((codes * scale).reshape(v.shape), -1, axis)


WIDE = False


def mx_kscale(k):
    if not WIDE:
        return np.ones(k)
    levels = np.array([30, -30])
    if k % 512:
        return np.exp2(np.random.permutation(np.resize(levels, k // 32))).repeat(32)
    a = np.empty((k // 512, 16))
    for p in range(k // 512):
        a[p, :8] = np.random.permutation(np.resize(levels, 8))
        for g in range(8):
            far = levels[np.abs(levels - a[p, g]) >= 10]
            a[p, g + 8] = far[np.random.randint(len(far))]
    return np.exp2(a.ravel()).repeat(32)


def f64(x):
    return np.asarray(x).astype(np.float64)


def striped(idx):
    return np.tile(np.asarray(idx).reshape(-1, 16).T, (8, 1)).astype(np.uint16)


def unstriped(offs):
    return offs[:16].T.reshape(-1).astype(np.int64)


E2M1 = np.array([0.0, 0.5, 1.0, 1.5, 2.0, 3.0, 4.0, 6.0, -0.0, -0.5, -1.0, -1.5, -2.0, -3.0, -4.0, -6.0])


def pack_weight(w, fmt):
    k, n = w.shape
    w = f64(np.asarray(w, np.float32).astype(ml_dtypes.bfloat16)).reshape(k // 32, 32, n)
    amax = np.abs(w).max(1)
    if fmt in ("e4m3", "e5m2"):
        byte = np.frexp(amax)[1] - 1 + 127 - (7 if fmt == "e4m3" else 14)
    else:
        mant, ex = np.frexp(amax / 6.0)
        byte = np.where(mant > 0.5, ex, ex - 1) + 127
    byte = np.clip(np.where(amax > 0, byte, 1), 1, 254)
    scaled = (w * np.exp2(127.0 - byte)[:, None, :]).reshape(k, n).astype(np.float32)
    by_word = np.ascontiguousarray(scaled.reshape(k // 512, 128, 4, n).transpose(0, 1, 3, 2))
    if fmt in ("e4m3", "e5m2"):
        words = by_word.astype(ml_dtypes.float8_e4m3fn if fmt == "e4m3" else ml_dtypes.float8_e5m2).view(np.uint8)
    else:
        c = by_word.astype(ml_dtypes.float4_e2m1fn).view(np.uint8) & 0xF
        words = (c[..., 0::2] | (c[..., 1::2] << 4)).reshape(k // 512, 128, 2 * n)
    return np.ascontiguousarray(words), np.ascontiguousarray(byte.astype(np.uint8).reshape(k // 512, 16, n))


def unpack_weight(words, scales, fmt):
    g, _, n = scales.shape
    words = np.ascontiguousarray(words).reshape(g, 128, n, -1)
    if fmt in ("e4m3", "e5m2"):
        vals = words.view(ml_dtypes.float8_e4m3fn if fmt == "e4m3" else ml_dtypes.float8_e5m2).astype(np.float64)
    else:
        nib = np.empty((g, 128, n, 4), np.uint8)
        nib[..., 0::2] = words & 0xF
        nib[..., 1::2] = words >> 4
        vals = E2M1[nib]
    vals = vals * np.repeat(np.exp2(scales.astype(np.float64) - 127.0), 8, axis=1)[..., None]
    return vals.transpose(0, 1, 3, 2).reshape(g * 512, n)


K, T, Z, J, R, C, N, E = 512, 1024, 1024, 256, 512, 512, 256, 128


def setup_inputs():
    n = np.random.standard_normal
    idx = np.random.permutation(T)[:J]
    idx2 = np.random.permutation(Z)[:J]
    idx3 = np.random.permutation(C)[:J]
    idx4 = np.random.permutation(C)[:J]
    idx5 = np.random.permutation(J)[:E]
    idx6 = np.random.permutation(J)[:E]
    fk = mx_kscale(K)
    fr = mx_kscale(R)
    xtp = pack_weight(n((K, T)) / fk[:, None], "e4m3")
    xop = pack_weight(n((K, Z)) / fk[:, None], "e2m1")
    wp = pack_weight(n((K, R)) * 1 / np.sqrt(K) * fk[:, None] * fr, "e5m2")
    w2p = pack_weight(n((K, R)) * 1 / np.sqrt(K) * fk[:, None] * fr, "e5m2")
    wbp = pack_weight(n((R, N)) * 1 / np.sqrt(R) / fr[:, None], "e5m2")
    return {
        "xt_words": xtp[0],
        "xt_scales": xtp[1],
        "xo_words": xop[0],
        "xo_scales": xop[1],
        "w_words": wp[0],
        "w_scales": wp[1],
        "w2_words": w2p[0],
        "w2_scales": w2p[1],
        "wb_words": wbp[0],
        "wb_scales": wbp[1],
        "offs": striped(idx),
        "offs2": striped(idx2),
        "offs3": striped(idx3),
        "offs4": striped(idx4),
        "offs5": striped(idx5),
        "offs6": striped(idx6),
    }


def reference(xt_words, xt_scales, xo_words, xo_scales, w_words, w_scales, w2_words, w2_scales, wb_words, wb_scales, offs, offs2, offs3, offs4, offs5, offs6):
    idx = unstriped(offs)
    idx2 = unstriped(offs2)
    idx3 = unstriped(offs3)
    idx4 = unstriped(offs4)
    idx5 = unstriped(offs5)
    idx6 = unstriped(offs6)
    xtu = unpack_weight(xt_words, xt_scales, "e4m3")
    xou = unpack_weight(xo_words, xo_scales, "e2m1")
    wu = unpack_weight(w_words, w_scales, "e5m2")
    w2u = unpack_weight(w2_words, w2_scales, "e5m2")
    wbu = unpack_weight(wb_words, wb_scales, "e5m2")
    xtidxg = xtu[:, idx]
    xoidx2g = xou[:, idx2]
    a = wu.T @ xtidxg + w2u.T @ xoidx2g
    b = w2u.T @ xtidxg + wu.T @ xoidx2g
    pw = np.zeros((R, C))
    pw[:, idx3] = a
    hid = np.abs(pw[:, idx4] - b)
    hidq = mxq(hid, 0, "e4m3")
    p = wbu.T @ hidq
    y = np.maximum(p[:, idx5], p[:, idx6])
    return y

@@ -1,0 +1,219 @@
+from contextlib import ExitStack
+
+import concourse.mybir as mybir
+
+K, T, Z, J, R, C, N, E = 512, 1024, 1024, 256, 512, 512, 256, 128
+FLOPS = 2 * (4 * K * R * J + R * N * J)
+
+F32 = mybir.dt.float32
+BF16 = mybir.dt.bfloat16
+I32 = mybir.dt.int32
+U32 = mybir.dt.uint32
+U16 = mybir.dt.uint16
+U8 = mybir.dt.uint8
+E4M3X4 = mybir.dt.float8_e4m3fn_x4
+E5M2X4 = mybir.dt.float8_e5m2_x4
+E2M1X4 = mybir.dt.float4_e2m1fn_x4
+ACT = mybir.ActivationFunctionType
+ALU = mybir.AluOpType
+
+P = 128
+PACK = 4
+QUADS = 4
+
+
+def tile_list_crossed_board_one_bestoftwo_kernel(
+    tc, xt_words, xt_scales, xo_words, xo_scales, w_words, w_scales, w2_words, w2_scales,
+    wb_words, wb_scales, offs, offs2, offs3, offs4, offs5, offs6, out,
+):
+    nc = tc.nc
+    with ExitStack() as ctx:
+        keep = ctx.enter_context(tc.tile_pool(name="keep", bufs=1))
+        psum = ctx.enter_context(tc.psum_pool(name="psum", bufs=1))
+
+        def sb(name, shape, dtype):
+            return keep.tile(shape, dtype, name=name, align_bytes=64)
+
+        def load_list(name, src):
+            lst = keep.tile(list(src.shape), U16, name=name)
+            nc.sync.dma_start(lst[:], src)
+            return lst
+
+        def load_words(name, src, cols, queue):
+            words = sb(name, [P, cols], I32)
+            queue.dma_start(out=words[:], in_=src[0].rearrange("p n t -> p (n t)").bitcast(I32))
+            return words
+
+        def zeroed_scales(name, cols):
+            scales = sb(name, [P, cols], U8)
+            nc.vector.memset(scales[:].bitcast(I32), 0)
+            return scales
+
+        def load_scales(scales, src, queue, quads=range(QUADS)):
+            for q in quads:
+                queue.dma_start(
+                    out=scales[32 * q : 32 * q + 4, :].bitcast(I32),
+                    in_=src[0, 4 * q : 4 * q + 4, :].bitcast(I32),
+                )
+
+        xt_s = zeroed_scales("xt_s", T)
+        xo_s = zeroed_scales("xo_s", Z)
+        ww_s = zeroed_scales("ww_s", 2 * R)
+        wb_s = zeroed_scales("wb_s", N)
+
+        l_tok = load_list("l_tok", offs)
+        l_note = load_list("l_note", offs2)
+        load_scales(xt_s, xt_scales, nc.sync)
+        xt_w = load_words("xt_w", xt_words, T, nc.sync)
+        xo_w = sb("xo_w", [P, Z], U16)
+        nc.sync.dma_start(out=xo_w[:].bitcast(I32), in_=xo_words[0].bitcast(I32))
+        load_scales(xo_s, xo_scales, nc.sync)
+        load_scales(ww_s[:, 0:R], w_scales, nc.sync, range(0, 2))
+        w_w = load_words("w_w", w_words, R, nc.sync)
+        w2_w = load_words("w2_w", w2_words, R, nc.sync)
+        load_scales(ww_s[:, 0:R], w_scales, nc.sync, range(2, 4))
+        load_scales(ww_s[:, R : 2 * R], w2_scales, nc.sync)
+        l_put = load_list("l_put", offs3)
+        l_get = load_list("l_get", offs4)
+        wb_w = load_words("wb_w", wb_words, N, nc.sync)
+        load_scales(wb_s, wb_scales, nc.sync)
+        l_first = load_list("l_first", offs5)
+        l_second = load_list("l_second", offs6)
+
+        board = [sb(f"board{t}", [P, C], F32) for t in range(PACK)]
+        for t in range(PACK):
+            nc.vector.memset(board[t][:], 0.0)
+
+        def deal_words(name, words, u):
+            dw = sb(name, [P, 2, P], U32)
+            nc.scalar.copy(
+                out=dw[:].rearrange("p t m -> p m t"),
+                in_=words[:].bitcast(U32).rearrange("p (m t) -> p m t", t=PACK)[:, :, 2 * u : 2 * u + 2],
+            )
+            return dw
+
+        def deal_scales(name, u):
+            ds = sb(name, [P, 2, 2, P], U8)
+            nc.vector.tensor_copy(
+                out=ds[:].rearrange("p w t m -> p w m t"),
+                in_=ww_s[:].rearrange("p (w m t) -> p w m t", w=2, t=PACK)[:, :, :, 2 * u : 2 * u + 2],
+            )
+            return ds
+
+        tok_w = sb("tok_w", [P, J], U32)
+        tok_s = sb("tok_s", [P, J], U8)
+        nc.vector.tensor_copy(tok_s[:], xt_s[:].indirect(l_tok[:]))
+        nc.vector.tensor_copy(tok_w[:], xt_w[:].bitcast(U32).indirect(l_tok[:]))
+        note_w = sb("note_w", [P, J], U16)
+        note_s = sb("note_s", [P, J], U8)
+        nc.vector.tensor_copy(note_w[:], xo_w[:].indirect(l_note[:]))
+        nc.vector.tensor_copy(note_s[:], xo_s[:].indirect(l_note[:]))
+        w_dw = [deal_words(f"w_dw{u}", w_w, u) for u in range(2)]
+        w2_dw = [deal_words(f"w2_dw{u}", w2_w, u) for u in range(2)]
+        ds = [deal_scales(f"ds{u}", u) for u in range(2)]
+        w_d = (w_dw, 0)
+        w2_d = (w2_dw, 1)
+
+        tok = (tok_w[:].bitcast(E4M3X4), tok_s[:])
+        note = (note_w[:].bitcast(E2M1X4), note_s[:])
+
+        def mx_pass(bank, weight, t, moving, first):
+            nc.tensor.matmul_mx(
+                out=bank[:],
+                lhsT=weight[0][t // 2][:, t % 2, :].bitcast(E5M2X4),
+                lhsT_scale=ds[t // 2][:, weight[1], t % 2, :],
+                rhs=moving[0],
+                rhs_scale=moving[1],
+                start=first,
+                stop=not first,
+            )
+
+        a_ps = [psum.tile([P, J], F32, name=f"a_ps{t}", tag=f"bank{t}") for t in range(PACK)]
+        b_ps = [psum.tile([P, J], F32, name=f"b_ps{t}", tag=f"bank{PACK + t}") for t in range(PACK)]
+        for t in range(PACK):
+            mx_pass(a_ps[t], w_d, t, tok, True)
+            mx_pass(a_ps[t], w2_d, t, note, False)
+        for t in range(PACK):
+            mx_pass(b_ps[t], w2_d, t, tok, True)
+            mx_pass(b_ps[t], w_d, t, note, False)
+
+        a_sb = [sb(f"a_sb{t}", [P, J], F32) for t in range(PACK)]
+        got = [sb(f"got{t}", [P, J], F32) for t in range(PACK)]
+        diff = [sb(f"diff{u}", [P, 2, J], F32) for u in range(2)]
+        hid = sb("hid", [P, J, PACK], BF16)
+
+        def on_vector(dst, src):
+            nc.vector.tensor_copy(dst, src)
+
+        def on_scalar(dst, src):
+            nc.scalar.activation(dst, src, ACT.Copy)
+
+        move = [on_vector, on_scalar, on_vector, on_scalar]
+
+        def subtract(t):
+            nc.vector.tensor_tensor(diff[t // 2][:, t % 2, :], got[t][:], b_ps[t][:], ALU.subtract)
+
+        def magnitude_scalar(u, js):
+            nc.scalar.activation(
+                hid[:, js, 2 * u : 2 * u + 2], diff[u][:, :, js].rearrange("p t j -> p j t"), ACT.Abs
+            )
+
+        def magnitude_vector(u, js):
+            d = diff[u][:, :, js].rearrange("p t j -> p j t")
+            nc.vector.scalar_tensor_tensor(hid[:, js, 2 * u : 2 * u + 2], d, -1.0, d, ALU.mult, ALU.max)
+
+        def evacuate(t):
+            move[t](a_sb[t][:], a_ps[t][:])
+
+        def put(t):
+            move[t](board[t][:].indirect(l_put[:]), a_sb[t][:])
+
+        def get(t):
+            move[t](got[t][:], board[t][:].indirect(l_get[:]))
+
+        for t in (0, 1):
+            evacuate(t)
+            put(t)
+            evacuate(t + 2)
+            get(t)
+            put(t + 2)
+        subtract(0)
+        subtract(1)
+        get(2)
+        get(3)
+        subtract(2)
+        subtract(3)
+        magnitude_scalar(0, slice(0, J))
+        magnitude_vector(1, slice(0, J // 2))
+        magnitude_scalar(1, slice(J // 2, J))
+
+        hid_w = sb("hid_w", [P, J], U32)
+        hid_s = sb("hid_s", [P, J], U8)
+        nc.vector.quantize_mx(
+            out=hid_w[:].bitcast(E4M3X4), scales=hid_s[:], in_=hid[:].rearrange("p j t -> p (j t)")
+        )
+
+        halves = N // P
+        p_sb = [sb(f"p_sb{h}", [P, J], F32) for h in range(halves)]
+        first = [sb(f"first{h}", [P, E], F32) for h in range(halves)]
+        second = [sb(f"second{h}", [P, E], F32) for h in range(halves)]
+        best = [sb(f"best{h}", [P, E], F32) for h in range(halves)]
+        p_ps = [psum.tile([P, J], F32, name=f"p_ps{h}", tag=f"bank{h}") for h in range(halves)]
+        for h in range(halves):
+            cols = slice(h * P, (h + 1) * P)
+            nc.tensor.matmul_mx(
+                out=p_ps[h][:],
+                lhsT=wb_w[:, cols].bitcast(E5M2X4),
+                lhsT_scale=wb_s[:, cols],
+                rhs=hid_w[:].bitcast(E4M3X4),
+                rhs_scale=hid_s[:],
+                start=True,
+                stop=True,
+            )
+        for h in range(halves):
+            move[h](p_sb[h][:], p_ps[h][:])
+            move[h](first[h][:], p_sb[h][:].indirect(l_first[:]))
+            move[h](second[h][:], p_sb[h][:].indirect(l_second[:]))
+        for h in range(halves):
+            nc.vector.tensor_tensor(best[h][:], first[h][:], second[h][:], ALU.max)
+            nc.sync.dma_start(out=out[h * P : (h + 1) * P, :], in_=best[h][:])

@@ -57,22 +57,24 @@ def tile_list_crossed_board_one_bestoftwo_kernel(
                 )
 
         xt_s = zeroed_scales("xt_s", T)
+        w_s = zeroed_scales("w_s", R)
         xo_s = zeroed_scales("xo_s", Z)
-        ww_s = zeroed_scales("ww_s", 2 * R)
+        w2_s = zeroed_scales("w2_s", R)
         wb_s = zeroed_scales("wb_s", N)
 
         l_tok = load_list("l_tok", offs)
         l_note = load_list("l_note", offs2)
         load_scales(xt_s, xt_scales, nc.sync)
+        load_scales(w_s, w_scales, nc.sync, range(0, 1))
         xt_w = load_words("xt_w", xt_words, T, nc.sync)
+        load_scales(w_s, w_scales, nc.sync, range(1, 4))
+        load_scales(xo_s, xo_scales, nc.sync, range(0, 2))
+        w_w = load_words("w_w", w_words, R, nc.sync)
         xo_w = sb("xo_w", [P, Z], U16)
         nc.sync.dma_start(out=xo_w[:].bitcast(I32), in_=xo_words[0].bitcast(I32))
-        load_scales(xo_s, xo_scales, nc.sync)
-        load_scales(ww_s[:, 0:R], w_scales, nc.sync, range(0, 2))
-        w_w = load_words("w_w", w_words, R, nc.sync)
         w2_w = load_words("w2_w", w2_words, R, nc.sync)
-        load_scales(ww_s[:, 0:R], w_scales, nc.sync, range(2, 4))
-        load_scales(ww_s[:, R : 2 * R], w2_scales, nc.sync)
+        load_scales(xo_s, xo_scales, nc.sync, range(2, 4))
+        load_scales(w2_s, w2_scales, nc.sync)
         l_put = load_list("l_put", offs3)
         l_get = load_list("l_get", offs4)
         wb_w = load_words("wb_w", wb_words, N, nc.sync)
@@ -84,35 +86,36 @@ def tile_list_crossed_board_one_bestoftwo_kernel(
         for t in range(PACK):
             nc.vector.memset(board[t][:], 0.0)
 
-        def deal_words(name, words, u):
-            dw = sb(name, [P, 2, P], U32)
+        def deal_words(name, words):
+            dealt = sb(name, [P, PACK, P], U32)
             nc.scalar.copy(
-                out=dw[:].rearrange("p t m -> p m t"),
-                in_=words[:].bitcast(U32).rearrange("p (m t) -> p m t", t=PACK)[:, :, 2 * u : 2 * u + 2],
+                out=dealt[:].rearrange("p t m -> p m t"),
+                in_=words[:].bitcast(U32).rearrange("p (m t) -> p m t", t=PACK),
             )
-            return dw
+            return [dealt[:, t, :] for t in range(PACK)]
 
-        def deal_scales(name, u):
-            ds = sb(name, [P, 2, 2, P], U8)
-            nc.vector.tensor_copy(
-                out=ds[:].rearrange("p w t m -> p w m t"),
-                in_=ww_s[:].rearrange("p (w m t) -> p w m t", w=2, t=PACK)[:, :, :, 2 * u : 2 * u + 2],
-            )
-            return ds
+        def deal_scales(name, scales, step):
+            planes = {}
+            for first in range(step):
+                dealt = sb(f"{name}{first}", [P, PACK // step, P], U8)
+                nc.vector.tensor_copy(
+                    out=dealt[:].rearrange("p t m -> p m t"),
+                    in_=scales[:].rearrange("p (m t) -> p m t", t=PACK)[:, :, first::step],
+                )
+                for i, t in enumerate(range(first, PACK, step)):
+                    planes[t] = dealt[:, i, :]
+            return planes
 
         tok_w = sb("tok_w", [P, J], U32)
         tok_s = sb("tok_s", [P, J], U8)
-        nc.vector.tensor_copy(tok_s[:], xt_s[:].indirect(l_tok[:]))
-        nc.vector.tensor_copy(tok_w[:], xt_w[:].bitcast(U32).indirect(l_tok[:]))
         note_w = sb("note_w", [P, J], U16)
         note_s = sb("note_s", [P, J], U8)
+        nc.vector.tensor_copy(tok_s[:], xt_s[:].indirect(l_tok[:]))
+        nc.vector.tensor_copy(tok_w[:], xt_w[:].bitcast(U32).indirect(l_tok[:]))
+        w_d = (deal_words("w_dw", w_w), deal_scales("w_ds", w_s, 1))
         nc.vector.tensor_copy(note_w[:], xo_w[:].indirect(l_note[:]))
         nc.vector.tensor_copy(note_s[:], xo_s[:].indirect(l_note[:]))
-        w_dw = [deal_words(f"w_dw{u}", w_w, u) for u in range(2)]
-        w2_dw = [deal_words(f"w2_dw{u}", w2_w, u) for u in range(2)]
-        ds = [deal_scales(f"ds{u}", u) for u in range(2)]
-        w_d = (w_dw, 0)
-        w2_d = (w2_dw, 1)
+        w2_d = (deal_words("w2_dw", w2_w), deal_scales("w2_ds", w2_s, 2))
 
         tok = (tok_w[:].bitcast(E4M3X4), tok_s[:])
         note = (note_w[:].bitcast(E2M1X4), note_s[:])
@@ -120,8 +123,8 @@ def tile_list_crossed_board_one_bestoftwo_kernel(
         def mx_pass(bank, weight, t, moving, first):
             nc.tensor.matmul_mx(
                 out=bank[:],
-                lhsT=weight[0][t // 2][:, t % 2, :].bitcast(E5M2X4),
-                lhsT_scale=ds[t // 2][:, weight[1], t % 2, :],
+                lhsT=weight[0][t].bitcast(E5M2X4),
+                lhsT_scale=weight[1][t],
                 rhs=moving[0],
                 rhs_scale=moving[1],
                 start=first,
@@ -130,8 +133,9 @@ def tile_list_crossed_board_one_bestoftwo_kernel(
 
         a_ps = [psum.tile([P, J], F32, name=f"a_ps{t}", tag=f"bank{t}") for t in range(PACK)]
         b_ps = [psum.tile([P, J], F32, name=f"b_ps{t}", tag=f"bank{PACK + t}") for t in range(PACK)]
-        for t in range(PACK):
+        for t in (0, 2, 1, 3):
             mx_pass(a_ps[t], w_d, t, tok, True)
+        for t in (0, 2, 1, 3):
             mx_pass(a_ps[t], w2_d, t, note, False)
         for t in range(PACK):
             mx_pass(b_ps[t], w2_d, t, tok, True)
@@ -140,7 +144,8 @@ def tile_list_crossed_board_one_bestoftwo_kernel(
         a_sb = [sb(f"a_sb{t}", [P, J], F32) for t in range(PACK)]
         got = [sb(f"got{t}", [P, J], F32) for t in range(PACK)]
         diff = [sb(f"diff{u}", [P, 2, J], F32) for u in range(2)]
-        hid = sb("hid", [P, J, PACK], BF16)
+        HALF = J // 2
+        hid = [sb(f"hid{g}", [P, HALF, PACK], BF16) for g in range(2)]
 
         def on_vector(dst, src):
             nc.vector.tensor_copy(dst, src)
@@ -148,22 +153,22 @@ def tile_list_crossed_board_one_bestoftwo_kernel(
         def on_scalar(dst, src):
             nc.scalar.activation(dst, src, ACT.Copy)
 
-        move = [on_vector, on_scalar, on_vector, on_scalar]
+        move = [on_vector, on_vector, on_scalar, on_scalar]
+        tail = [on_vector, on_scalar]
 
         def subtract(t):
             nc.vector.tensor_tensor(diff[t // 2][:, t % 2, :], got[t][:], b_ps[t][:], ALU.subtract)
 
-        def magnitude_scalar(u, js):
-            nc.scalar.activation(
-                hid[:, js, 2 * u : 2 * u + 2], diff[u][:, :, js].rearrange("p t j -> p j t"), ACT.Abs
-            )
+        def magnitude_scalar(u, g):
+            d = diff[u][:, :, g * HALF : (g + 1) * HALF].rearrange("p t j -> p j t")
+            nc.scalar.activation(hid[g][:, :, 2 * u : 2 * u + 2], d, ACT.Abs)
 
-        def magnitude_vector(u, js):
-            d = diff[u][:, :, js].rearrange("p t j -> p j t")
-            nc.vector.scalar_tensor_tensor(hid[:, js, 2 * u : 2 * u + 2], d, -1.0, d, ALU.mult, ALU.max)
+        def magnitude_vector(u, g):
+            d = diff[u][:, :, g * HALF : (g + 1) * HALF].rearrange("p t j -> p j t")
+            nc.vector.scalar_tensor_tensor(hid[g][:, :, 2 * u : 2 * u + 2], d, -1.0, d, ALU.mult, ALU.max)
 
-        def evacuate(t):
-            move[t](a_sb[t][:], a_ps[t][:])
+        def evacuate(t, how):
+            how(a_sb[t][:], a_ps[t][:])
 
         def put(t):
             move[t](board[t][:].indirect(l_put[:]), a_sb[t][:])
@@ -171,49 +176,50 @@ def tile_list_crossed_board_one_bestoftwo_kernel(
         def get(t):
             move[t](got[t][:], board[t][:].indirect(l_get[:]))
 
-        for t in (0, 1):
-            evacuate(t)
+        evacuate(0, on_vector)
+        for t in (2, 1, 3):
+            evacuate(t, on_scalar)
+        for t in range(PACK):
             put(t)
-            evacuate(t + 2)
+        for t in range(PACK):
             get(t)
-            put(t + 2)
-        subtract(0)
-        subtract(1)
-        get(2)
-        get(3)
-        subtract(2)
-        subtract(3)
-        magnitude_scalar(0, slice(0, J))
-        magnitude_vector(1, slice(0, J // 2))
-        magnitude_scalar(1, slice(J // 2, J))
-
-        hid_w = sb("hid_w", [P, J], U32)
-        hid_s = sb("hid_s", [P, J], U8)
-        nc.vector.quantize_mx(
-            out=hid_w[:].bitcast(E4M3X4), scales=hid_s[:], in_=hid[:].rearrange("p j t -> p (j t)")
-        )
+        for t in range(PACK):
+            subtract(t)
+        magnitude_scalar(0, 0)
+        magnitude_scalar(0, 1)
+        magnitude_vector(1, 0)
+        magnitude_scalar(1, 1)
 
         halves = N // P
+        hid_w = [sb(f"hid_w{g}", [P, HALF], U32) for g in range(2)]
+        hid_s = [sb(f"hid_s{g}", [P, HALF], U8) for g in range(2)]
         p_sb = [sb(f"p_sb{h}", [P, J], F32) for h in range(halves)]
         first = [sb(f"first{h}", [P, E], F32) for h in range(halves)]
         second = [sb(f"second{h}", [P, E], F32) for h in range(halves)]
         best = [sb(f"best{h}", [P, E], F32) for h in range(halves)]
-        p_ps = [psum.tile([P, J], F32, name=f"p_ps{h}", tag=f"bank{h}") for h in range(halves)]
-        for h in range(halves):
-            cols = slice(h * P, (h + 1) * P)
-            nc.tensor.matmul_mx(
-                out=p_ps[h][:],
-                lhsT=wb_w[:, cols].bitcast(E5M2X4),
-                lhsT_scale=wb_s[:, cols],
-                rhs=hid_w[:].bitcast(E4M3X4),
-                rhs_scale=hid_s[:],
-                start=True,
-                stop=True,
+        for g in range(2):
+            nc.vector.quantize_mx(
+                out=hid_w[g][:].bitcast(E4M3X4),
+                scales=hid_s[g][:],
+                in_=hid[g][:].rearrange("p j t -> p (j t)"),
             )
+        for g in range(2):
+            for h in range(halves):
+                cols = slice(h * P, (h + 1) * P)
+                p_ps = psum.tile([P, HALF], F32, name=f"p_ps{g}{h}", tag=f"bank{2 * g + h}")
+                nc.tensor.matmul_mx(
+                    out=p_ps[:],
+                    lhsT=wb_w[:, cols].bitcast(E5M2X4),
+                    lhsT_scale=wb_s[:, cols],
+                    rhs=hid_w[g][:].bitcast(E4M3X4),
+                    rhs_scale=hid_s[g][:],
+                    start=True,
+                    stop=True,
+                )
+                tail[h](p_sb[h][:, g * HALF : (g + 1) * HALF], p_ps[:])
         for h in range(halves):
-            move[h](p_sb[h][:], p_ps[h][:])
-            move[h](first[h][:], p_sb[h][:].indirect(l_first[:]))
-            move[h](second[h][:], p_sb[h][:].indirect(l_second[:]))
+            tail[h](first[h][:], p_sb[h][:].indirect(l_first[:]))
+            tail[h](second[h][:], p_sb[h][:].indirect(l_second[:]))
         for h in range(halves):
             nc.vector.tensor_tensor(best[h][:], first[h][:], second[h][:], ALU.max)
             nc.sync.dma_start(out=out[h * P : (h + 1) * P, :], in_=best[h][:])

@@ -56,24 +56,24 @@ def tile_list_crossed_board_one_bestoftwo_kernel(
                     in_=src[0, 4 * q : 4 * q + 4, :].bitcast(I32),
                 )
 
+        xo_s = zeroed_scales("xo_s", Z)
         xt_s = zeroed_scales("xt_s", T)
         w_s = zeroed_scales("w_s", R)
-        xo_s = zeroed_scales("xo_s", Z)
         w2_s = zeroed_scales("w2_s", R)
         wb_s = zeroed_scales("wb_s", N)
 
+        load_scales(xo_s, xo_scales, nc.gpsimd, range(1, 4))
         l_tok = load_list("l_tok", offs)
         l_note = load_list("l_note", offs2)
         load_scales(xt_s, xt_scales, nc.sync)
         load_scales(w_s, w_scales, nc.sync, range(0, 1))
         xt_w = load_words("xt_w", xt_words, T, nc.sync)
         load_scales(w_s, w_scales, nc.sync, range(1, 4))
-        load_scales(xo_s, xo_scales, nc.sync, range(0, 2))
+        load_scales(xo_s, xo_scales, nc.sync, range(0, 1))
         w_w = load_words("w_w", w_words, R, nc.sync)
         xo_w = sb("xo_w", [P, Z], U16)
         nc.sync.dma_start(out=xo_w[:].bitcast(I32), in_=xo_words[0].bitcast(I32))
         w2_w = load_words("w2_w", w2_words, R, nc.sync)
-        load_scales(xo_s, xo_scales, nc.sync, range(2, 4))
         load_scales(w2_s, w2_scales, nc.sync)
         l_put = load_list("l_put", offs3)
         l_get = load_list("l_get", offs4)
@@ -84,27 +84,26 @@ def tile_list_crossed_board_one_bestoftwo_kernel(
 
         board = [sb(f"board{t}", [P, C], F32) for t in range(PACK)]
         for t in range(PACK):
-            nc.vector.memset(board[t][:], 0.0)
+            nc.vector.memset(board[t][:, 0 : C // 2 + 1], 0.0)
+            nc.vector.memset(board[t][:, C // 2 + 1 : C], 0.0)
 
-        def deal_words(name, words):
-            dealt = sb(name, [P, PACK, P], U32)
-            nc.scalar.copy(
-                out=dealt[:].rearrange("p t m -> p m t"),
-                in_=words[:].bitcast(U32).rearrange("p (m t) -> p m t", t=PACK),
-            )
-            return [dealt[:, t, :] for t in range(PACK)]
-
-        def deal_scales(name, scales, step):
+        def deal(name, src, dtype, copy, step):
             planes = {}
             for first in range(step):
-                dealt = sb(f"{name}{first}", [P, PACK // step, P], U8)
-                nc.vector.tensor_copy(
+                dealt = sb(f"{name}{first}", [P, PACK // step, P], dtype)
+                copy(
                     out=dealt[:].rearrange("p t m -> p m t"),
-                    in_=scales[:].rearrange("p (m t) -> p m t", t=PACK)[:, :, first::step],
+                    in_=src.rearrange("p (m t) -> p m t", t=PACK)[:, :, first::step],
                 )
                 for i, t in enumerate(range(first, PACK, step)):
                     planes[t] = dealt[:, i, :]
             return planes
+
+        def deal_words(name, words, step):
+            return deal(name, words[:].bitcast(U32), U32, nc.scalar.copy, step)
+
+        def deal_scales(name, scales, step):
+            return deal(name, scales[:], U8, nc.vector.tensor_copy, step)
 
         tok_w = sb("tok_w", [P, J], U32)
         tok_s = sb("tok_s", [P, J], U8)
@@ -112,10 +111,10 @@ def tile_list_crossed_board_one_bestoftwo_kernel(
         note_s = sb("note_s", [P, J], U8)
         nc.vector.tensor_copy(tok_s[:], xt_s[:].indirect(l_tok[:]))
         nc.vector.tensor_copy(tok_w[:], xt_w[:].bitcast(U32).indirect(l_tok[:]))
-        w_d = (deal_words("w_dw", w_w), deal_scales("w_ds", w_s, 1))
+        w_d = (deal_words("w_dw", w_w, 1), deal_scales("w_ds", w_s, 1))
         nc.vector.tensor_copy(note_w[:], xo_w[:].indirect(l_note[:]))
         nc.vector.tensor_copy(note_s[:], xo_s[:].indirect(l_note[:]))
-        w2_d = (deal_words("w2_dw", w2_w), deal_scales("w2_ds", w2_s, 2))
+        w2_d = (deal_words("w2_dw", w2_w, 2), deal_scales("w2_ds", w2_s, 2))
 
         tok = (tok_w[:].bitcast(E4M3X4), tok_s[:])
         note = (note_w[:].bitcast(E2M1X4), note_s[:])
@@ -156,8 +155,8 @@ def tile_list_crossed_board_one_bestoftwo_kernel(
         move = [on_vector, on_vector, on_scalar, on_scalar]
         tail = [on_vector, on_scalar]
 
-        def subtract(t):
-            nc.vector.tensor_tensor(diff[t // 2][:, t % 2, :], got[t][:], b_ps[t][:], ALU.subtract)
+        def subtract(t, js):
+            nc.vector.tensor_tensor(diff[t // 2][:, t % 2, js], got[t][:, js], b_ps[t][:, js], ALU.subtract)
 
         def magnitude_scalar(u, g):
             d = diff[u][:, :, g * HALF : (g + 1) * HALF].rearrange("p t j -> p j t")
@@ -183,8 +182,10 @@ def tile_list_crossed_board_one_bestoftwo_kernel(
             put(t)
         for t in range(PACK):
             get(t)
-        for t in range(PACK):
-            subtract(t)
+        for t in range(PACK - 1):
+            subtract(t, slice(0, J))
+        for g in range(2):
+            subtract(PACK - 1, slice(g * HALF, (g + 1) * HALF))
         magnitude_scalar(0, 0)
         magnitude_scalar(0, 1)
         magnitude_vector(1, 0)

@@ -56,25 +56,70 @@ def tile_list_crossed_board_one_bestoftwo_kernel(
                     in_=src[0, 4 * q : 4 * q + 4, :].bitcast(I32),
                 )
 
-        xo_s = zeroed_scales("xo_s", Z)
-        xt_s = zeroed_scales("xt_s", T)
+        def load_rows(scales, src):
+            nc.sync.dma_start(out=scales[0:16, :].bitcast(I32), in_=src[0].bitcast(I32))
+
         w_s = zeroed_scales("w_s", R)
+        xt_s = zeroed_scales("xt_s", T)
+        xo_s = zeroed_scales("xo_s", Z)
         w2_s = zeroed_scales("w2_s", R)
         wb_s = zeroed_scales("wb_s", N)
+        board = [sb(f"board{t}", [P, C], F32) for t in range(PACK)]
+        for t in range(PACK):
+            nc.vector.memset(board[t][:], 0.0)
 
-        load_scales(xo_s, xo_scales, nc.gpsimd, range(1, 4))
         l_tok = load_list("l_tok", offs)
+        load_rows(w_s, w_scales)
+        load_rows(xt_s, xt_scales)
         l_note = load_list("l_note", offs2)
-        load_scales(xt_s, xt_scales, nc.sync)
-        load_scales(w_s, w_scales, nc.sync, range(0, 1))
+        load_rows(xo_s, xo_scales)
+        load_rows(w2_s, w2_scales)
         xt_w = load_words("xt_w", xt_words, T, nc.sync)
-        load_scales(w_s, w_scales, nc.sync, range(1, 4))
-        load_scales(xo_s, xo_scales, nc.sync, range(0, 1))
         w_w = load_words("w_w", w_words, R, nc.sync)
         xo_w = sb("xo_w", [P, Z], U16)
         nc.sync.dma_start(out=xo_w[:].bitcast(I32), in_=xo_words[0].bitcast(I32))
         w2_w = load_words("w2_w", w2_words, R, nc.sync)
-        load_scales(w2_s, w2_scales, nc.sync)
+
+        def deal_words(name, words, step):
+            planes = {}
+            for first in range(step):
+                dealt = sb(f"{name}{first}", [P, PACK // step, P], U32)
+                nc.scalar.copy(
+                    out=dealt[:].rearrange("p t m -> p m t"),
+                    in_=words[:].bitcast(U32).rearrange("p (m t) -> p m t", t=PACK)[:, :, first::step],
+                )
+                for i, t in enumerate(range(first, PACK, step)):
+                    planes[t] = dealt[:, i, :]
+            return planes
+
+        def pick_scales(name, table, lst):
+            picked = sb(name, [P, J], U8)
+            nc.vector.tensor_copy(picked[:], table[:].indirect(lst[:]))
+            return picked
+
+        def deal_scales(planes, weight):
+            nc.vector.tensor_copy(
+                out=planes[:, J:].rearrange("p (t m) -> p m t", t=PACK),
+                in_=weight[:].rearrange("p (m t) -> p m t", t=PACK),
+            )
+
+        def spread(planes, picked):
+            nc.vector.tensor_copy(planes[:, 0:J].bitcast(I32), picked[:].bitcast(I32))
+            for q in range(1, QUADS):
+                nc.sync.dma_start(
+                    out=planes[32 * q : 32 * q + 4, :].bitcast(I32),
+                    in_=planes[4 * q : 4 * q + 4, :].bitcast(I32),
+                )
+            return planes[:, 0:J], [planes[:, J + t * P : J + (t + 1) * P] for t in range(PACK)]
+
+        tok_planes = sb("tok_planes", [P, J + R], U8)
+        note_planes = sb("note_planes", [P, J + R], U8)
+        deal_scales(tok_planes, w_s)
+        tok_s, w_ds = spread(tok_planes, pick_scales("tok_picked", xt_s, l_tok))
+        note_picked = pick_scales("note_picked", xo_s, l_note)
+        deal_scales(note_planes, w2_s)
+        note_s, w2_ds = spread(note_planes, note_picked)
+
         l_put = load_list("l_put", offs3)
         l_get = load_list("l_get", offs4)
         wb_w = load_words("wb_w", wb_words, N, nc.sync)
@@ -82,42 +127,15 @@ def tile_list_crossed_board_one_bestoftwo_kernel(
         l_first = load_list("l_first", offs5)
         l_second = load_list("l_second", offs6)
 
-        board = [sb(f"board{t}", [P, C], F32) for t in range(PACK)]
-        for t in range(PACK):
-            nc.vector.memset(board[t][:, 0 : C // 2 + 1], 0.0)
-            nc.vector.memset(board[t][:, C // 2 + 1 : C], 0.0)
-
-        def deal(name, src, dtype, copy, step):
-            planes = {}
-            for first in range(step):
-                dealt = sb(f"{name}{first}", [P, PACK // step, P], dtype)
-                copy(
-                    out=dealt[:].rearrange("p t m -> p m t"),
-                    in_=src.rearrange("p (m t) -> p m t", t=PACK)[:, :, first::step],
-                )
-                for i, t in enumerate(range(first, PACK, step)):
-                    planes[t] = dealt[:, i, :]
-            return planes
-
-        def deal_words(name, words, step):
-            return deal(name, words[:].bitcast(U32), U32, nc.scalar.copy, step)
-
-        def deal_scales(name, scales, step):
-            return deal(name, scales[:], U8, nc.vector.tensor_copy, step)
-
         tok_w = sb("tok_w", [P, J], U32)
-        tok_s = sb("tok_s", [P, J], U8)
         note_w = sb("note_w", [P, J], U16)
-        note_s = sb("note_s", [P, J], U8)
-        nc.vector.tensor_copy(tok_s[:], xt_s[:].indirect(l_tok[:]))
         nc.vector.tensor_copy(tok_w[:], xt_w[:].bitcast(U32).indirect(l_tok[:]))
-        w_d = (deal_words("w_dw", w_w, 1), deal_scales("w_ds", w_s, 1))
         nc.vector.tensor_copy(note_w[:], xo_w[:].indirect(l_note[:]))
-        nc.vector.tensor_copy(note_s[:], xo_s[:].indirect(l_note[:]))
-        w2_d = (deal_words("w2_dw", w2_w, 2), deal_scales("w2_ds", w2_s, 2))
+        w_d = (deal_words("w_dw", w_w, 1), w_ds)
+        w2_d = (deal_words("w2_dw", w2_w, 2), w2_ds)
 
-        tok = (tok_w[:].bitcast(E4M3X4), tok_s[:])
-        note = (note_w[:].bitcast(E2M1X4), note_s[:])
+        tok = (tok_w[:].bitcast(E4M3X4), tok_s)
+        note = (note_w[:].bitcast(E2M1X4), note_s)
 
         def mx_pass(bank, weight, t, moving, first):
             nc.tensor.matmul_mx(

from contextlib import ExitStack

import concourse.mybir as mybir

K, T, Z, J, R, C, N, E = 512, 1024, 1024, 256, 512, 512, 256, 128
FLOPS = 2 * (4 * K * R * J + R * N * J)

F32 = mybir.dt.float32
BF16 = mybir.dt.bfloat16
I32 = mybir.dt.int32
U32 = mybir.dt.uint32
U16 = mybir.dt.uint16
U8 = mybir.dt.uint8
E4M3X4 = mybir.dt.float8_e4m3fn_x4
E5M2X4 = mybir.dt.float8_e5m2_x4
E2M1X4 = mybir.dt.float4_e2m1fn_x4
ACT = mybir.ActivationFunctionType
ALU = mybir.AluOpType

P = 128
PACK = 4
QUADS = 4


def tile_list_crossed_board_one_bestoftwo_kernel(
    tc, xt_words, xt_scales, xo_words, xo_scales, w_words, w_scales, w2_words, w2_scales,
    wb_words, wb_scales, offs, offs2, offs3, offs4, offs5, offs6, out,
):
    nc = tc.nc
    with ExitStack() as ctx:
        keep = ctx.enter_context(tc.tile_pool(name="keep", bufs=1))
        psum = ctx.enter_context(tc.psum_pool(name="psum", bufs=1))

        def sb(name, shape, dtype):
            return keep.tile(shape, dtype, name=name, align_bytes=64)

        def load_list(name, src):
            lst = keep.tile(list(src.shape), U16, name=name)
            nc.sync.dma_start(lst[:], src)
            return lst

        def load_words(name, src, cols, queue):
            words = sb(name, [P, cols], I32)
            queue.dma_start(out=words[:], in_=src[0].rearrange("p n t -> p (n t)").bitcast(I32))
            return words

        def zeroed_scales(name, cols):
            scales = sb(name, [P, cols], U8)
            nc.vector.memset(scales[:].bitcast(I32), 0)
            return scales

        def load_scales(scales, src, queue, quads=range(QUADS)):
            for q in quads:
                queue.dma_start(
                    out=scales[32 * q : 32 * q + 4, :].bitcast(I32),
                    in_=src[0, 4 * q : 4 * q + 4, :].bitcast(I32),
                )

        def load_rows(scales, src):
            nc.sync.dma_start(out=scales[0:16, :].bitcast(I32), in_=src[0].bitcast(I32))

        w_s = zeroed_scales("w_s", R)
        xt_s = zeroed_scales("xt_s", T)
        xo_s = zeroed_scales("xo_s", Z)
        w2_s = zeroed_scales("w2_s", R)
        wb_s = zeroed_scales("wb_s", N)
        board = [sb(f"board{t}", [P, C], F32) for t in range(PACK)]
        for t in range(PACK):
            nc.vector.memset(board[t][:], 0.0)

        l_tok = load_list("l_tok", offs)
        load_rows(w_s, w_scales)
        load_rows(xt_s, xt_scales)
        l_note = load_list("l_note", offs2)
        load_rows(xo_s, xo_scales)
        load_rows(w2_s, w2_scales)
        xt_w = load_words("xt_w", xt_words, T, nc.sync)
        w_w = load_words("w_w", w_words, R, nc.sync)
        xo_w = sb("xo_w", [P, Z], U16)
        nc.sync.dma_start(out=xo_w[:].bitcast(I32), in_=xo_words[0].bitcast(I32))
        w2_w = load_words("w2_w", w2_words, R, nc.sync)

        def deal_words(name, words, step):
            planes = {}
            for first in range(step):
                dealt = sb(f"{name}{first}", [P, PACK // step, P], U32)
                nc.scalar.copy(
                    out=dealt[:].rearrange("p t m -> p m t"),
                    in_=words[:].bitcast(U32).rearrange("p (m t) -> p m t", t=PACK)[:, :, first::step],
                )
                for i, t in enumerate(range(first, PACK, step)):
                    planes[t] = dealt[:, i, :]
            return planes

        def pick_scales(name, table, lst):
            picked = sb(name, [P, J], U8)
            nc.vector.tensor_copy(picked[:], table[:].indirect(lst[:]))
            return picked

        def deal_scales(planes, weight):
            nc.vector.tensor_copy(
                out=planes[:, J:].rearrange("p (t m) -> p m t", t=PACK),
                in_=weight[:].rearrange("p (m t) -> p m t", t=PACK),
            )

        def spread(planes, picked):
            nc.vector.tensor_copy(planes[:, 0:J].bitcast(I32), picked[:].bitcast(I32))
            for q in range(1, QUADS):
                nc.sync.dma_start(
                    out=planes[32 * q : 32 * q + 4, :].bitcast(I32),
                    in_=planes[4 * q : 4 * q + 4, :].bitcast(I32),
                )
            return planes[:, 0:J], [planes[:, J + t * P : J + (t + 1) * P] for t in range(PACK)]

        tok_planes = sb("tok_planes", [P, J + R], U8)
        note_planes = sb("note_planes", [P, J + R], U8)
        deal_scales(tok_planes, w_s)
        tok_s, w_ds = spread(tok_planes, pick_scales("tok_picked", xt_s, l_tok))
        note_picked = pick_scales("note_picked", xo_s, l_note)
        deal_scales(note_planes, w2_s)
        note_s, w2_ds = spread(note_planes, note_picked)

        l_put = load_list("l_put", offs3)
        l_get = load_list("l_get", offs4)
        wb_w = load_words("wb_w", wb_words, N, nc.sync)
        load_scales(wb_s, wb_scales, nc.sync)
        l_first = load_list("l_first", offs5)
        l_second = load_list("l_second", offs6)

        tok_w = sb("tok_w", [P, J], U32)
        note_w = sb("note_w", [P, J], U16)
        nc.vector.tensor_copy(tok_w[:], xt_w[:].bitcast(U32).indirect(l_tok[:]))
        nc.vector.tensor_copy(note_w[:], xo_w[:].indirect(l_note[:]))
        w_d = (deal_words("w_dw", w_w, 1), w_ds)
        w2_d = (deal_words("w2_dw", w2_w, 2), w2_ds)

        tok = (tok_w[:].bitcast(E4M3X4), tok_s)
        note = (note_w[:].bitcast(E2M1X4), note_s)

        def mx_pass(bank, weight, t, moving, first):
            nc.tensor.matmul_mx(
                out=bank[:],
                lhsT=weight[0][t].bitcast(E5M2X4),
                lhsT_scale=weight[1][t],
                rhs=moving[0],
                rhs_scale=moving[1],
                start=first,
                stop=not first,
            )

        a_ps = [psum.tile([P, J], F32, name=f"a_ps{t}", tag=f"bank{t}") for t in range(PACK)]
        b_ps = [psum.tile([P, J], F32, name=f"b_ps{t}", tag=f"bank{PACK + t}") for t in range(PACK)]
        for t in (0, 2, 1, 3):
            mx_pass(a_ps[t], w_d, t, tok, True)
        for t in (0, 2, 1, 3):
            mx_pass(a_ps[t], w2_d, t, note, False)
        for t in range(PACK):
            mx_pass(b_ps[t], w2_d, t, tok, True)
            mx_pass(b_ps[t], w_d, t, note, False)

        a_sb = [sb(f"a_sb{t}", [P, J], F32) for t in range(PACK)]
        got = [sb(f"got{t}", [P, J], F32) for t in range(PACK)]
        diff = [sb(f"diff{u}", [P, 2, J], F32) for u in range(2)]
        HALF = J // 2
        hid = [sb(f"hid{g}", [P, HALF, PACK], BF16) for g in range(2)]

        def on_vector(dst, src):
            nc.vector.tensor_copy(dst, src)

        def on_scalar(dst, src):
            nc.scalar.activation(dst, src, ACT.Copy)

        move = [on_vector, on_vector, on_scalar, on_scalar]
        tail = [on_vector, on_scalar]

        def subtract(t, js):
            nc.vector.tensor_tensor(diff[t // 2][:, t % 2, js], got[t][:, js], b_ps[t][:, js], ALU.subtract)

        def magnitude_scalar(u, g):
            d = diff[u][:, :, g * HALF : (g + 1) * HALF].rearrange("p t j -> p j t")
            nc.scalar.activation(hid[g][:, :, 2 * u : 2 * u + 2], d, ACT.Abs)

        def magnitude_vector(u, g):
            d = diff[u][:, :, g * HALF : (g + 1) * HALF].rearrange("p t j -> p j t")
            nc.vector.scalar_tensor_tensor(hid[g][:, :, 2 * u : 2 * u + 2], d, -1.0, d, ALU.mult, ALU.max)

        def evacuate(t, how):
            how(a_sb[t][:], a_ps[t][:])

        def put(t):
            move[t](board[t][:].indirect(l_put[:]), a_sb[t][:])

        def get(t):
            move[t](got[t][:], board[t][:].indirect(l_get[:]))

        evacuate(0, on_vector)
        for t in (2, 1, 3):
            evacuate(t, on_scalar)
        for t in range(PACK):
            put(t)
        for t in range(PACK):
            get(t)
        for t in range(PACK - 1):
            subtract(t, slice(0, J))
        for g in range(2):
            subtract(PACK - 1, slice(g * HALF, (g + 1) * HALF))
        magnitude_scalar(0, 0)
        magnitude_scalar(0, 1)
        magnitude_vector(1, 0)
        magnitude_scalar(1, 1)

        halves = N // P
        hid_w = [sb(f"hid_w{g}", [P, HALF], U32) for g in range(2)]
        hid_s = [sb(f"hid_s{g}", [P, HALF], U8) for g in range(2)]
        p_sb = [sb(f"p_sb{h}", [P, J], F32) for h in range(halves)]
        first = [sb(f"first{h}", [P, E], F32) for h in range(halves)]
        second = [sb(f"second{h}", [P, E], F32) for h in range(halves)]
        best = [sb(f"best{h}", [P, E], F32) for h in range(halves)]
        for g in range(2):
            nc.vector.quantize_mx(
                out=hid_w[g][:].bitcast(E4M3X4),
                scales=hid_s[g][:],
                in_=hid[g][:].rearrange("p j t -> p (j t)"),
            )
        for g in range(2):
            for h in range(halves):
                cols = slice(h * P, (h + 1) * P)
                p_ps = psum.tile([P, HALF], F32, name=f"p_ps{g}{h}", tag=f"bank{2 * g + h}")
                nc.tensor.matmul_mx(
                    out=p_ps[:],
                    lhsT=wb_w[:, cols].bitcast(E5M2X4),
                    lhsT_scale=wb_s[:, cols],
                    rhs=hid_w[g][:].bitcast(E4M3X4),
                    rhs_scale=hid_s[g][:],
                    start=True,
                    stop=True,
                )
                tail[h](p_sb[h][:, g * HALF : (g + 1) * HALF], p_ps[:])
        for h in range(halves):
            tail[h](first[h][:], p_sb[h][:].indirect(l_first[:]))
            tail[h](second[h][:], p_sb[h][:].indirect(l_second[:]))
        for h in range(halves):
            nc.vector.tensor_tensor(best[h][:], first[h][:], second[h][:], ALU.max)
            nc.sync.dma_start(out=out[h * P : (h + 1) * P, :], in_=best[h][:])
